import numpy as np, ml_dtypes
CORES = [36,164,52,180,100,228,116,244]
N = 8
BF = ml_dtypes.bfloat16
M, L, KH, CAP, RO, OC = 4096, 512, 8, 64, 3, 1024
S = 8
def pack(b, o, w):
    return {"ball": np.ascontiguousarray(b.reshape(N, 128, M)).astype(np.float32).astype(BF), "stk": np.ascontiguousarray(o.reshape(N, 128, L)).astype(np.int32),
            "wt": np.ascontiguousarray(w.reshape(N, 128, 1)).astype(np.float32).astype(BF)}
def halves(rng):
    bright = np.argsort(rng.random((N, 8, M)), axis=-1) < M // 2
    return np.where(bright[:, :, None], rng.integers(140, 256, (N, 8, 16, M)), rng.integers(0, 120, (N, 8, 16, M))), bright
def stacks(rng, kk, bright):
    br, di = np.flatnonzero(bright), np.flatnonzero(~bright); dep = np.arange(16)[:, None]
    o = rng.integers(0, M, (16, L)); top = np.where(kk > 0, rng.choice(br, L), rng.choice(di, L))
    o = np.where((dep > 0) & (dep <= kk), rng.choice(di, (16, L)), o)
    o = np.where(dep == kk + 1, np.where(kk > 0, top, rng.choice(br, L)), o)
    o[0] = top
    return o
def later(rng, z):
    kk = np.concatenate([np.full(L // 2, 15), np.zeros(z, np.int64), rng.integers(1, KH, L - L // 2 - z)])
    kk[:int(np.sum(kk)) % S] = 14
    kk = rng.permutation(kk); dep = np.arange(16)[:, None]
    kind = rng.permutation(np.arange(M - L) % 3)
    b = rng.integers(0, 256, (16, M))
    b[:, L:] = np.where(kind == 0, rng.integers(0, 40, (16, M - L)), np.where(kind == 1, rng.integers(60, 200, (16, M - L)), 255))
    low, mid, top = L + np.flatnonzero(kind == 0), L + np.flatnonzero(kind == 1), L + np.flatnonzero(kind == 2)
    o = np.where((dep > 0) & (dep <= kk), rng.choice(mid, (16, L)), rng.integers(0, M, (16, L)))
    o = np.where(dep == kk + 1, rng.choice(top, (16, L)), o)
    o[0] = rng.choice(low, L)
    return b, o
def quiet(rng, a):
    c = np.arange(M) // L; free = rng.permutation(np.flatnonzero((c > 0) & (c != a)))
    low, top = free[:16], free[16:M // 2]
    b = rng.integers(0, 256, (16, M)); b[:, low] = 0; b[:, top] = 255
    o = rng.integers(0, M, (16, L)); one = rng.permutation(L) < a
    o[0] = np.where(one, rng.choice(top, L), o[0]); o[1] = np.where(one, rng.choice(low, L), rng.choice(top, L)); o[2] = np.where(one, rng.choice(top, L), o[2])
    return b, o
def setup_inputs(rng):
    lev = rng.integers(0, 256, (N, 8, 1, M))
    b = np.clip(lev + np.rint(24 * rng.standard_normal((N, 8, 16, M), dtype=np.float32)).astype(np.int64), 0, 255)
    o = rng.integers(0, M, (N, 8, 16, L)); high = np.argsort(lev[:, :, 0], axis=-1)[..., M - M // 8:]
    pick = np.take_along_axis(high, rng.integers(0, M // 8, (N, 8, L)), 2); share = rng.choice(np.array([0.0, 0.1, 0.3, 0.5]), (N, 8, 1))
    o[:, :, 0] = np.where(rng.random((N, 8, L)) < share, pick, o[:, :, 0])
    return pack(b, o, rng.integers(0, 256, (N, 8, 16, 1)))
def setup_inputs_room(rng):
    b, bright = halves(rng); o = np.zeros((N, 8, 16, L), np.int64); c = np.array([0, 1, CAP - 1, CAP, CAP + 1, L])
    for q in range(N):
        for g in range(8):
            n, z = int(rng.choice(c)), int(rng.choice(c))
            if q in (0, 2): n = (CAP, CAP + 1, L, CAP - 1, 1, 0, CAP, CAP + 1)[g]
            if q in (1, 3):
                z = (CAP, CAP + 1, CAP, CAP, 0, L, CAP - 1, 1)[g]; n = min(n, L - z)
            z = min(z, L - n)
            kk = np.concatenate([rng.choice(np.array([KH, KH, KH + 1, 15]), n), np.zeros(z, np.int64), rng.choice(np.array([1, KH // 2, KH - 1, KH - 1]), L - n - z)])
            kk = rng.permutation(kk)
            if q in (0, 2) and g == 0:
                i = int(np.flatnonzero(kk >= KH)[0]); kk[[i, L - 1]] = kk[[L - 1, i]]
            if q in (1, 3) and g < 3: kk = kk[np.argsort(kk > 0, kind="stable")]
            o[q, g] = stacks(rng, kk, bright[q, g])
    return pack(b, o, rng.integers(0, 256, (N, 8, 16, 1)))
def setup_inputs_votes(rng):
    base = rng.integers(1, 255, (N, 8, 16, 1)); j = rng.choice(np.array([7, 8, 9, 10, 16]), (N, 8, 1, M), p=[0.04, 0.06, 0.5, 0.2, 0.2])
    place = np.argsort(rng.random((N, 8, 16, M)), axis=2)
    b = base - (place < j) + (place >= j) * rng.integers(0, 2, (N, 8, 16, M))
    b[..., ::4] = base
    o = 4 * rng.integers(0, M // 4, (N, 8, 16, L)) + rng.integers(1, 4, (N, 8, 16, L))
    o[:, :, 0] = np.where(rng.random((N, 8, L)) < 0.7, 4 * rng.integers(0, M // 4, (N, 8, L)), o[:, :, 0])
    return pack(b, o, rng.integers(0, 256, (N, 8, 16, 1)))
def setup_inputs_ends(rng):
    b, bright = halves(rng); b[..., 0] = 255; b[..., M - 1] = 0; bright[..., 0] = True; bright[..., M - 1] = False
    b[:, 4, :, 1023] = 255; b[:, 4, :, M - 16] = 0; bright[:, 4, 1023] = True; bright[:, 4, M - 16] = False
    o = np.zeros((N, 8, 16, L), np.int64); w = rng.integers(0, 256, (N, 8, 16, 1)); w[:, 0::2] = 255; w[:, 1] = 0; w[:, 5:] = 0
    for q in range(N):
        for g in range(8):
            kk = rng.integers(0, 16, L); kk[0] = 15 * (q % 2); kk[L - 1] = 15 * (1 - q % 2)
            if g == 4: kk[:] = 15
            if g == 6: b[q, g], o[q, g] = quiet(rng, int(rng.integers(1, S)))
            elif g in (5, 7): b[q, g], o[q, g] = later(rng, (0, 1, CAP // 2, CAP - 1)[(q + g) % 4])
            else: o[q, g] = stacks(rng, kk, bright[q, g])
    o[:, 0] = rng.choice(np.array([M - 1, M - 1, M - 1, M - 1, M - 1, M - 1, 0]), (N, 16, L))
    o[:, 0, 0] = rng.choice(np.array([0, 0, M - 1]), (N, L))
    o[:, 2] = o[:, 2, :1]
    far = np.where(np.arange(16)[:, None] == 0, 1023, rng.choice(np.array([M - 1, M - 16]), (N, 16, L)))
    o[:, 4] = np.where(rng.random((N, 1, L)) < 0.25, far, o[:, 4])
    return pack(b, o, w)
def setup_inputs_spread(rng):
    b = np.minimum(np.exp2(8.5 * rng.random((N, 8, 1, M))) * rng.random((N, 8, 16, M)), 255.0).astype(np.int64) * (rng.random((N, 8, 1, M)) > 0.0625)
    w = np.exp2(8 * rng.random((N, 8, 16, 1))).astype(np.int64) - 1
    o = (M * rng.random((N, 8, 16, L)) ** rng.choice(np.array([1, 2, 4]), (N, 8, 1, 1))).astype(np.int64)
    return pack(b, o, w)
def check_inputs(d):
    bad = []
    for k, hi in (("ball", 255), ("stk", M - 1), ("wt", 255)):
        v = np.asarray(d[k]).astype(np.float64)
        if not (np.min(v) >= 0 and np.max(v) <= hi): bad.append("range of " + k)
        elif np.any(v != np.floor(v)): bad.append("whole numbers in " + k)
    return bad
def reference(ball, stk, wt):
    b = ball.astype(np.float32).astype(np.int64).reshape(N, 8, 16, M)
    o = stk.astype(np.int64).reshape(N, 8, 16, L)
    w = wt.astype(np.float32).astype(np.int64).reshape(N, 8, 16, 1)
    lane = np.arange(L); dep = np.arange(16)[:, None]
    for t in range(RO):
        p = np.take_along_axis(b, o.reshape(N, 8, 1, 16 * L), 3).reshape(N, 8, 16, 16, L)
        x, rest = p[:, :, :, 0], p[:, :, :, 1:]
        won = np.add.reduce((x[:, :, :, None] > rest).astype(np.int64), axis=2) >= 9
        crossed = np.multiply.accumulate(won.astype(np.int64), axis=2)
        k = np.add.reduce(crossed, axis=2)
        top = np.where(k[:, :, None] == 0, 255, np.max(rest * crossed[:, :, None], axis=3))
        y = np.abs(x - top)
        A = np.add.reduce(k, axis=2)
        v = L * ((np.add.reduce(w * y, axis=2) + A[:, :, None]) & (S - 1)) + lane
        new = (((o * (2 * (o[:, :, :1] & 1023) + 1)) >> 4) + A[:, :, None, None]) & (M - 1)
        up = np.concatenate([new[:, :, 1:], new[:, :, :1]], axis=2)
        o = np.where(dep < k[:, :, None], up, np.where(dep == k[:, :, None], v[:, :, None], o))
        z = y.copy()
        for r in range(N):
            q = (r - 1 - t) % N
            for g in range(8):
                src = np.flatnonzero(k[q, g] >= KH)[:CAP]; dst = np.flatnonzero(k[r, g] == 0)[:len(src)]
                z[r, g][:, dst] = y[q, g][:, src[:len(dst)]]
        np.put_along_axis(b, v[:, :, None, :], z, 3)
    return {"yo": o.reshape(N, 128, L).astype(np.float32), "yb": b.reshape(N, 128, M)[:, :, :OC].astype(np.float32).astype(BF)}

from concourse.mybir import AluOpType, ActivationFunctionType

F, B, I, U = "float32", "bfloat16", "int32", "uint16"


def sb(n, d):
    return ("sbuf", [128, n], d)


SCRATCH = {
    "bl": sb(4160, B), "P": sb(8192, B), "PM": sb(8192, B), "C": sb(3840, B),
    "si": sb(512, I), "off": sb(512, U), "o": sb(512, F), "w": sb(1, B),
    "ci": sb(1, I), "cgi": sb(1, I), "cai": sb(1, I), "cG": sb(1, F), "cA": sb(1, F), "cP": sb(1, F), "dh": sb(1, F), "dm": sb(1, F),
    "c15": sb(1, F), "c16": sb(1, F), "z0": sb(1, F), "wi": sb(1, I), "wf": sb(1, F),
    "rG": sb(128, B), "rA": sb(128, B), "rP": sb(144, F), "r8": sb(8, B), "dd16": sb(2048, B),
    "BO": sb(128, B), "BOf": sb(128, F), "M16": sb(128, B), "ID": sb(128, B), "IDf": sb(128, F), "TRI": sb(128, B),
    "UP": sb(128, B), "W": sb(144, B), "SHf": sb(128, F), "SHn": sb(128, B), "SHI": sb(128, B), "BC0": sb(128, F),
    "BCn": sb(128, B), "WS": sb(128, B), "DBn": sb(8, B), "DBf": sb(8, F), "RM": sb(2048, B), "R16": sb(128, B), "RR": sb(64, B),
    "ones": sb(512, B), "hi": sb(512, B), "lo": sb(512, B), "r256": sb(8, B), "a16": sb(128, B), "lt15": sb(128, B), "e15": sb(128, B),
    "iw": sb(32, F), "il": sb(32, F), "il8": sb(32, F), "ix": sb(32, F), "cpos": sb(64, F), "nd": sb(4, F), "LN": sb(512, F),
    "DF": sb(64, F), "rr": sb(64, F),
    "fl": sb(512, B), "E2": sb(512, F), "T1": sb(512, I), "q": sb(512, I), "qA": sb(512, F), "Xn": sb(512, F), "tt": sb(512, F),
    "Ui": sb(512, I), "sg": sb(512, B), "nX": sb(512, B), "acc": sb(4, F), "km": sb(512, B), "lu": sb(32, U),
    "df": sb(512, B), "y": sb(576, B), "ym": sb(512, F), "Rr": sb(576, F), "A": sb(1, F), "A5": sb(1, F), "FZ": sb(64, B),
    "sc": sb(64, F), "ri": sb(64, F), "tm": sb(64, F), "po": sb(32, F), "pu": sb(32, U), "IDb": sb(1536, F),
    "idm": sb(128, F), "ids": sb(128, F), "idu": sb(4, U), "idv": sb(4, U), "iwA": sb(32, F), "vi": sb(32, I),
    "vu": sb(32, U), "zf": sb(4, F), "cb": sb(4, F), "cc": sb(4, F), "Rz": sb(64, F), "zm": sb(64, F), "zs": sb(64, F), "zi": sb(4, I),
    "zo": sb(4, F), "zu": sb(4, U),
}
for _t in range(3):
    SCRATCH["ty%d" % _t] = sb(64, B)
    SCRATCH["ry%d" % _t] = sb(64, B)
    SCRATCH["tf%d" % _t] = sb(4, F)
    SCRATCH["rf%d" % _t] = sb(4, F)
for _b in range(8):
    SCRATCH["b%d" % _b] = ("psum", [128, 512], F)

SEMAPHORES = ["sV", "sS", "sP", "sG", "dstk", "dball", "dwt", "dyo", "dyb", "loc"]
for _t in range(3):
    SEMAPHORES += ["aY%d" % _t, "aF%d" % _t]

PIECE = [(0, 64), (64, 128), (128, 256), (256, 384), (384, 512)]
VX = 160


def rank_program(g, core, T, topo):
    rank = T.rank_of(core)
    if rank is None:
        return
    N = len(T.cores)
    OP, ACT = AluOpType, ActivationFunctionType
    eng = {"V": g.vector, "S": g.scalar, "P": g.tensor, "G": g, "Y": g.sync}
    cnt = {}
    known = {q: {} for q in eng}
    clk = {}
    hist = {}

    def r(name, a=0, b=None, s=1, n=128):
        return (name, a, SCRATCH[name][1][1] if b is None else b, s, n)

    def ap(x):
        t = T[x[0]]
        if x[3] == 1:
            return t[:, x[1]:x[2]] if x[4] == 128 else t[0:x[4], x[1]:x[2]]
        return t[:, x[1]:x[2]:x[3]]

    def meet(x, y):
        if x[2] <= y[1] or y[2] <= x[1]:
            return False
        if x[3] == y[3] and x[3] > 1 and (x[1] - y[1]) % x[3]:
            return False
        return True

    def inside(x, y):
        return y[3] == 1 and y[1] <= x[1] and x[2] <= y[2]

    def learn(q, sem, n):
        k = known[q]
        for e, v in clk.get((sem, n), {sem: n}).items():
            if v > k.get(e, 0):
                k[e] = v

    def need(q, sem, n):
        if known[q].get(sem, 0) < n:
            eng[q].wait_ge(T.sem[sem], n)
            learn(q, sem, n)

    def deps(q, reads, writes, group=False):
        want = {}
        for x, w in [(x, False) for x in reads] + [(x, True) for x in writes]:
            psum = SCRATCH[x[0]][0] == "psum"
            for (q2, sem, n, y, w2) in hist.get(x[0], []):
                if q2 == q and (not w2 or group):
                    continue
                if not (q2 != q and psum) and (not (w or w2) or not meet(x, y)):
                    continue
                want[sem] = max(want.get(sem, 0), n)
        for sem in sorted(want, key=lambda e: -want[e]):
            need(q, sem, want[sem])

    def note(q, sem, n, reads, writes):
        for x, w in [(x, False) for x in reads] + [(x, True) for x in writes]:
            h = hist.setdefault(x[0], [])
            if w:
                psum = SCRATCH[x[0]][0] == "psum"
                h[:] = [e for e in h if not (inside(e[3], x) and (not psum or e[0] == q or known[q].get(e[1], 0) >= e[2]))]
            else:
                h[:] = [e for e in h if not (e[0] == q and not e[4] and e[3] == x)]
            h.append((q, sem, n, x, w))
        c = dict(known[q])
        c[sem] = n
        clk[(sem, n)] = c

    def op(q, reads, writes, call, group=False):
        deps(q, reads, writes, group)
        sem = "s" + q
        cnt[sem] = cnt.get(sem, 0) + 1
        call().then_inc(T.sem[sem], 1)
        note(q, sem, cnt[sem], reads, writes)

    def isr(x):
        return isinstance(x, tuple)

    def val(x):
        return ap(x) if isr(x) else x

    def tt(out, a, b, o):
        op("V", [a, b], [out], lambda: g.vector.tensor_tensor(ap(out), ap(a), ap(b), o))

    def ts(out, a, s1, o0, s2=None, o1=None):
        rd = [a] + [x for x in (s1, s2) if isr(x)]
        if o1 is None:
            op("V", rd, [out], lambda: g.vector.tensor_scalar(ap(out), ap(a), val(s1), None, o0))
        else:
            op("V", rd, [out], lambda: g.vector.tensor_scalar(ap(out), ap(a), val(s1), val(s2), o0, o1))

    def cp(out, a):
        op("V", [a], [out], lambda: g.vector.tensor_copy(ap(out), ap(a)))

    def ms(out, v):
        op("V", [], [out], lambda: g.vector.memset(ap(out), v))

    def scan(out, d0, d1, o0, o1):
        op("V", [d0, d1], [out], lambda: g.vector.tensor_tensor_scan(ap(out), ap(d0), ap(d1), 0.0, o0, o1))

    def act(out, a, f, bias=0.0, scale=1.0, acc=None):
        rd = [a] + [x for x in (bias, scale) if isr(x)]
        if acc is None:
            op("S", rd, [out], lambda: g.scalar.activation(ap(out), ap(a), f, bias=val(bias), scale=val(scale)))
        else:
            op("S", rd, [out, acc], lambda: g.scalar.activation(ap(out), ap(a), f, bias=val(bias), scale=val(scale), accum_out=ap(acc)))

    def mm(out, l, rhs, start=True, stop=True):
        op("P", [l, rhs], [out], lambda: g.tensor.matmul(ap(out), ap(l), ap(rhs), start, stop), group=not start)

    def iota(out, pat, base=0, cm=0):
        if SCRATCH[out[0]][2] == I:
            op("G", [], [out], lambda: g.iota(ap(out), pat, base, cm))
        else:
            op("G", [], [out], lambda: g.iota(ap(out), pat, base, cm, allow_small_or_imprecise_dtypes=True))

    def gather(q, out, win, offs):
        if q == "V":
            op("V", [win, offs], [out], lambda: g.vector.tensor_copy(ap(out), ap(win).indirect(ap(offs))))
        else:
            op("S", [win, offs], [out], lambda: g.scalar.activation(ap(out), ap(win).indirect(ap(offs)), ACT.Copy))

    def scatter(win, offs, a):
        op("V", [a, offs], [win], lambda: g.vector.tensor_copy(ap(win).indirect(ap(offs)), ap(a)))

    def dma(q, out, a, sem, rd, wr):
        deps(q, rd, wr)
        eng[q].dma_start(out, a).then_inc(T.sem[sem], 16)
        cnt[sem] = 16
        for x in rd:
            hist.setdefault(x[0], []).append((sem, sem, 16, x, False))
        for x in wr:
            hist.setdefault(x[0], []).append((sem, sem, 16, x, True))
        c = dict(known[q])
        c[sem] = 16
        clk[(sem, 16)] = c

    def send(src, dst_buf, to, sem):
        deps("G", [src], [])
        rid, pid = topo.addr(to, core)
        g.remote_dma(ap((dst_buf,) + src[1:]), ap(src), T.sem[sem], T.sem["loc"], pid, rid, topo.mask(core, to))
        cnt["loc"] = cnt.get("loc", 0) + len(topo.engines(core, to))

    dma("Y", ap(r("w")), T.wt[:, :], "dwt", [], [r("w")])
    dma("Y", ap(r("si")), T.stk[:, :], "dstk", [], [r("si")])
    dma("S", ap(r("bl", 0, 4096)), T.ball[:, :], "dball", [], [r("bl", 0, 4096)])

    iota(r("ci"), [[0, 1]], 0, 1)
    iota(r("rA"), [[0, 8], [1, 16]])
    iota(r("rG"), [[1, 8], [0, 16]])
    iota(r("rP"), [[1, 144]])
    iota(r("r8"), [[1, 8]])
    iota(r("r256"), [[256, 8]])
    iota(r("a16"), [[0, 8], [16, 16]], 15)
    iota(r("iw"), [[16, 32]])
    iota(r("il"), [[0, 4], [256, 8]])
    iota(r("rr"), [[0, 2], [1, 32]])
    iota(r("dd16"), [[0, 128], [1, 16]])
    iota(r("hi"), [[256, 2], [0, 256]])
    iota(r("lo"), [[0, 2], [1, 256]])
    iota(r("LN"), [[1, 512]], 32)
    iota(r("DF"), [[1, 64]], 544)
    ms(r("ones"), 1.0)
    ms(r("y", 512, 576), 0.0)
    ms(r("Rr", 512, 576), 0.0)
    ts(r("cgi"), r("ci"), 4, OP.arith_shift_right)
    ts(r("cai"), r("ci"), 15, OP.bitwise_and)
    cp(r("cG"), r("cgi"))
    cp(r("cA"), r("cai"))
    cp(r("cP"), r("ci"))
    ts(r("BO"), r("rG"), r("cG"), OP.is_equal)
    cp(r("BOf"), r("BO"))
    ts(r("M16"), r("rA"), r("cA"), OP.is_equal)
    tt(r("ID"), r("BO"), r("M16"), OP.mult)
    cp(r("IDf"), r("ID"))
    ts(r("dh"), r("cA"), 0.5, OP.mult)
    ts(r("dm"), r("cA"), 1.0, OP.is_ge)
    ts(r("c15"), r("cG"), 16.0, OP.mult, 15.0, OP.add)
    ts(r("z0"), r("cA"), 0.0, OP.is_equal)
    ts(r("W"), r("rP"), r("c15"), OP.is_equal)
    ts(r("SHf"), r("rP", 1, 129), r("cP"), OP.is_equal, r("dm"), OP.mult)
    ts(r("SHn"), r("SHf"), -1.0, OP.mult)
    tt(r("SHI"), r("SHf"), r("ID"), OP.subtract)
    ts(r("BC0"), r("BO"), r("z0"), OP.mult, 2.0, OP.mult)
    ts(r("BCn"), r("BC0"), -1024.0, OP.mult)
    ts(r("TRI"), r("rA"), r("cA"), OP.is_ge, r("dm"), OP.mult)
    ts(r("TRI"), r("TRI"), 0.5, OP.mult)
    tt(r("TRI"), r("TRI"), r("BO"), OP.mult)
    ts(r("UP"), r("rA"), r("cA"), OP.is_lt, -1.0, OP.mult)
    tt(r("UP"), r("UP"), r("BO"), OP.mult)
    ts(r("DBn"), r("r8"), r("cG"), OP.is_equal, -1.0, OP.mult)
    ts(r("DBf"), r("r8"), r("cG"), OP.is_equal)
    ts(r("lt15"), r("rA"), 15.0, OP.is_lt)
    ts(r("e15"), r("rA"), 15.0, OP.is_equal)
    ts(r("R16"), r("rA"), 1.0, OP.is_ge)
    ts(r("RR"), r("rr"), 1.0, OP.is_ge)
    ts(r("iw"), r("iw"), r("cA"), OP.add)
    ts(r("c16"), r("cA"), 16.0, OP.mult)
    ts(r("il"), r("il"), r("c16"), OP.add)
    ts(r("il8"), r("il"), 8.0, OP.add)
    ts(r("ix"), r("iw"), 1024.0, OP.add)
    ts(r("cpos", 0, 32), r("iw"), -1.0, OP.mult, -1025.0, OP.add)
    ts(r("cpos", 32, 64), r("iw"), -1.0, OP.mult, -513.0, OP.add)
    ts(r("nd"), r("iw", 0, 4), 4096.0, OP.add)
    cp(r("off"), r("si"))
    ts(r("wi"), r("w"), 4.0, OP.add)
    ts(r("wi"), r("wi"), 7, OP.bitwise_and)
    ts(r("wf"), r("wi"), -4.0, OP.add, 512.0, OP.mult)
    ts(r("WS"), r("BO"), r("wf"), OP.mult)
    ts(r("RM"), r("dd16"), 2.0, OP.is_ge)

    def bank(n, a=0, b=512):
        return r("b%d" % n, a, b)

    def one(name, n):
        return r(name, 0, n, 1, 1)

    def gat(q, a, b):
        if b > a:
            gather(q, r("P", 16 * a, 16 * b), r("bl", 0, 4096), r("off", a, b))

    def cn(c, k):
        return bank(2 + c % 2, 128 * k, 128 * k + 128)

    def col(c, n=128):
        return n * c, n * c + n

    def xcopy(p):
        a, b = PIECE[p]
        mm(bank(p % 2, 0, b - a), r("ID"), r("P", 16 * a, 16 * b, 16))

    def comp(p):
        a, b = PIECE[p]
        c, n = a // 128, b - a
        for d in range(1, 16):
            k = 1920 * (c % 2) + 128 * (d - 1) + a % 128
            tt(r("C", k, k + n), r("P", 16 * a + d, 16 * b, 16), bank(p % 2, 0, n), OP.is_lt)
            mm(bank(2 + c % 2, a % 128, a % 128 + n), r("W", 15 - d, 143 - d), r("C", k, k + n), d == 1, d == 15)

    def pmax(c):
        a, b = col(c, 2048)
        scan(r("PM", a, b), r("RM"), r("P", a, b), OP.mult, OP.max)
        iota(r("PM", a, b, 16), [[0, 128]], 255)

    def vote(c):
        act(r("sg", *col(c)), cn(c, 0), ACT.Sign, bias=8.5, scale=-1.0)

    def tri(c):
        mm(cn(c, 1), r("TRI"), r("sg", *col(c)))

    def over(c):
        act(r("nX", *col(c)), cn(c, 1), ACT.Sign, bias=r("dh"), acc=r("acc", c, c + 1))

    def kexp(c):
        mm(bank(4, *col(c % 2)), r("nX", *col(c)), r("BO"))

    def kmask(c):
        tt(r("km", *col(c)), bank(4, *col(c % 2)), r("M16"), OP.mult)
        o = bank(5, *col(c, 8))
        mm(o, one("ones", 128), one("r256", 8), True, False)
        mm(o, one("a16", 128), one("ones", 8), False, False)
        mm(o, r("km", *col(c)), r("DBn"), False, True)

    def sel(c):
        cp(r("lu", *col(c, 8)), bank(5, *col(c, 8)))
        a, b = col(c, 2048)
        win, offs, x, out = r("PM", a, b), r("lu", *col(c, 8)), r("P", a, b, 16), r("df", *col(c))
        op("V", [win, offs, x], [out], lambda: g.vector.tensor_tensor(ap(out), ap(win).indirect(ap(offs)), ap(x), OP.subtract))

    def yabs(c):
        act(r("y", *col(c)), r("df", *col(c)), ACT.Abs)
        mm(cn(c, 2 + c // 2), r("y", *col(c)), r("WS"))

    def ymask(c):
        tt(r("ym", *col(c)), cn(c, 2 + c // 2), r("M16"), OP.mult)
        mm(bank(5, 192 + 8 * c, 200 + 8 * c), r("ym", *col(c)), r("DBf"))

    for t in range(3):
        last = t == 2
        to, frm = T.cores[(rank + t + 1) % N], T.cores[(rank - t - 1) % N]
        for name, sem in (("ry%d" % t, "aY%d" % t), ("rf%d" % t, "aF%d" % t)):
            n = len(topo.engines(frm, core))
            hist[name] = [(sem, sem, n, r(name), True)]
            cnt[sem] = n
        gat("V", 0, 32)
        gat("S", 32, 64)
        xcopy(0)
        gat("S", 64, 128)
        comp(0)
        cp(r("o"), r("Ui" if t else "si"))
        xcopy(1)
        gat("S", VX, 192)
        comp(1)
        gat("V", 128, VX)
        gat("S", 192, 256)
        pmax(0)
        vote(0)
        xcopy(2)
        tri(0)
        mm(bank(7), r("SHf"), r("o"))
        act(r("fl"), r("o"), ACT.Identity, bias=128.5005, scale=1.0 / 1024)
        gat("S", 256, 320)
        over(0)
        comp(2)
        kexp(0)
        pmax(1)
        gat("S", 320, 384)
        xcopy(3)
        mm(bank(6), r("BC0"), r("o"), True, False)
        mm(bank(6), r("BCn"), r("fl"), False, True)
        vote(1)
        tri(1)
        gat("S", 384, 448)
        over(1)
        kmask(0)
        comp(3)
        kexp(1)
        pmax(2)
        sel(0)
        kmask(1)
        gat("S", 448, 512)
        xcopy(4)
        vote(2)
        tri(2)
        over(2)
        yabs(0)
        act(r("E2"), bank(6), ACT.Identity, bias=float(2048 * 129 + 1))
        act(r("IDb", 0, 64), r("DF"), ACT.Silu)
        act(r("IDb", 512, 576), r("DF"), ACT.Silu)
        comp(4)
        kexp(2)
        vote(3)
        tri(3)
        over(3)
        sel(1)
        tt(r("T1"), bank(7), r("E2"), OP.mult)
        kmask(2)
        kexp(3)
        yabs(1)
        sel(2)
        kmask(3)
        yabs(2)
        tt(r("FZ", 0, 32), bank(5, 0, 32), r("il8"), OP.is_ge)
        tt(r("FZ", 32, 64), bank(5, 0, 32), r("il"), OP.is_equal)
        ts(r("q"), r("T1"), 4, OP.arith_shift_right)
        mm(bank(4, 256, 320), r("BO"), r("FZ"))
        mm(bank(4, 320, 384), r("IDf"), r("cpos"), True, False)
        mm(bank(4, 320, 384), r("UP"), r("FZ"), False, True)
        for c in range(4):
            mm(bank(5, 64, 65), r("BOf"), r("acc", c, c + 1), c == 0, c == 3)
        scan(r("sc"), r("RR"), bank(4, 256, 320), OP.mult, OP.add)
        tt(r("ri"), r("sc"), bank(4, 320, 384), OP.add)
        tt(r("tm"), r("ri"), r("FZ"), OP.mult)
        tt(r("po"), r("tm", 0, 32), r("tm", 32, 64), OP.add)
        tt(r("po"), r("po"), r("ix"), OP.add)
        cp(r("pu"), r("po"))
        op("S", [r("LN"), r("pu")], [r("IDb")],
           lambda: g.scalar.activation(ap(r("IDb")).indirect(ap(r("pu"))), ap(r("LN")), ACT.Silu))
        pmax(3)
        ts(r("tf%d" % t), r("iw", 0, 4), r("sc", 31, 32), OP.is_ge, 8192.0, OP.mult)
        send(r("tf%d" % t), "rf%d" % t, to, "aF%d" % t)
        ts(r("zf"), r("iw", 0, 4), r("sc", 63, 64), OP.is_ge, 8192.0, OP.mult)
        ts(r("A"), bank(5, 64, 65), -1.0, OP.mult, 7680.0, OP.add)
        ts(r("A5"), bank(5, 64, 65), -512.0, OP.mult, 512.0 * 7680.0, OP.add)
        ts(r("iwA"), r("iw"), r("A5"), OP.add)
        sel(3)
        mm(bank(7), r("ID"), r("nX"))
        mm(bank(6), r("SHn"), r("nX"), True, False)
        mm(bank(6), one("lt15", 128), one("ones", 512), False, True)
        mm(bank(1), one("ones", 128), one("hi", 512), True, False)
        mm(bank(1), one("ones", 128), one("lo", 512), False, False)
        yabs(3)
        mm(bank(1), r("WS"), r("y", 0, 512), False, True)
        act(r("Rr", 0, 512), bank(1), ACT.Identity, bias=r("A5"))
        ts(r("qA"), r("q"), r("A"), OP.add)
        tt(bank(7), bank(7), r("o"), OP.mult)
        tt(r("Xn"), bank(6), r("qA"), OP.mult)
        for c in range(4):
            ymask(c)
        mm(bank(0), r("SHI"), r("nX"), True, False)
        mm(bank(0), one("e15", 128), one("ones", 512), False, True)
        tt(r("vi"), bank(5, 192, 224), r("iwA"), OP.add)
        tt(r("idm", 0, 64), r("IDb", 0, 64), r("M16", 0, 64), OP.mult)
        scan(r("ids", 0, 64), r("R16", 0, 64), r("idm", 0, 64), OP.mult, OP.add)
        ts(r("idu", 0, 4), r("ids", 15, 64, 16), -31.75, OP.add)
        gather("S", r("ty%d" % t), r("y"), r("idu", 0, 4))
        send(r("ty%d" % t), "ry%d" % t, to, "aY%d" % t)
        ts(r("vi"), r("vi"), 4095, OP.bitwise_and)
        cp(r("vu"), r("vi"))
        tt(bank(7), bank(7), r("Xn"), OP.add)
        tt(r("tt"), bank(0), r("Rr", 0, 512), OP.mult)
        tt(r("idm", 64, 128), r("IDb", 512, 576), r("M16", 0, 64), OP.mult)
        scan(r("ids", 64, 128), r("R16", 64, 128), r("idm", 64, 128), OP.mult, OP.add)
        ts(r("idv", 0, 4), r("ids", 79, 128, 16), -31.75, OP.add)
        gather("S", r("Rz"), r("Rr"), r("idv", 0, 4))
        tt(r("Ui"), bank(7), r("tt"), OP.add)
        ts(r("Ui"), r("Ui"), 4095, OP.bitwise_and)
        if last:
            cp(r("o"), r("Ui"))
            dma("Y", T.yo[:, :], ap(r("o")), "dyo", [r("o")], [])
        else:
            cp(r("off"), r("Ui"))
        scatter(r("bl", 0, 4096), r("vu"), r("y", 0, 512))
        tt(r("zm"), r("Rz"), r("M16", 0, 64), OP.mult)
        scan(r("zs"), r("R16", 0, 64), r("zm"), OP.mult, OP.add)
        cp(r("zi"), r("zs", 15, 64, 16))
        ts(r("zi"), r("zi"), 4095, OP.bitwise_and)
        tt(r("cb"), r("zf"), r("rf%d" % t), OP.max)
        tt(r("cc"), r("cb"), r("nd"), OP.min)
        tt(r("zo"), r("zi"), r("cc"), OP.max)
        cp(r("zu"), r("zo"))
        scatter(r("bl"), r("zu"), r("ry%d" % t))
    dma("Y", T.yb[:, :], ap(r("bl", 0, 1024)), "dyb", [r("bl", 0, 1024)], [])
    for sem in cnt:
        need("Y", sem, cnt[sem])
